import numpy as np
import ml_dtypes


def mxq(x, axis, fmt="e4m3"):
    dtype, down = {"e4m3": (ml_dtypes.float8_e4m3fn, 7), "e5m2": (ml_dtypes.float8_e5m2, 14)}[fmt]
    v = np.moveaxis(np.asarray(x, np.float32).astype(ml_dtypes.bfloat16).astype(np.float64), axis, -1)
    blocks = v.reshape(v.shape[:-1] + (-1, 32))
    amax = np.abs(blocks).max(-1, keepdims=True)
    byte = np.maximum(np.where(amax > 0, np.frexp(amax)[1] - 1 + 127, 0) - down, 1)
    scale = np.exp2(byte - 127.0)
    codes = (blocks / scale).astype(np.float32).astype(dtype).astype(np.float64)
    return np.moveaxis((codes * scale).reshape(v.shape), -1, axis)


WIDE = False


def mx_kscale(k):
    if not WIDE:
        return np.ones(k)
    levels = np.array([30, -30])
    if k % 512:
        return np.exp2(np.random.permutation(np.resize(levels, k // 32))).repeat(32)
    a = np.empty((k // 512, 16))
    for p in range(k // 512):
        a[p, :8] = np.random.permutation(np.resize(levels, 8))
        for g in range(8):
            far = levels[np.abs(levels - a[p, g]) >= 10]
            a[p, g + 8] = far[np.random.randint(len(far))]
    return np.exp2(a.ravel()).repeat(32)


def f64(x):
    return np.asarray(x).astype(np.float64)


def striped(idx):
    return np.tile(np.asarray(idx).reshape(-1, 16).T, (8, 1)).astype(np.uint16)


def unstriped(offs):
    return offs[:16].T.reshape(-1).astype(np.int64)


E2M1 = np.array([0.0, 0.5, 1.0, 1.5, 2.0, 3.0, 4.0, 6.0, -0.0, -0.5, -1.0, -1.5, -2.0, -3.0, -4.0, -6.0])


def pack_weight(w, fmt):
    k, n = w.shape
    w = f64(np.asarray(w, np.float32).astype(ml_dtypes.bfloat16)).reshape(k // 32, 32, n)
    amax = np.abs(w).max(1)
    if fmt in ("e4m3", "e5m2"):
        byte = np.frexp(amax)[1] - 1 + 127 - (7 if fmt == "e4m3" else 14)
    else:
        mant, ex = np.frexp(amax / 6.0)
        byte = np.where(mant > 0.5, ex, ex - 1) + 127
    byte = np.clip(np.where(amax > 0, byte, 1), 1, 254)
    scaled = (w * np.exp2(127.0 - byte)[:, None, :]).reshape(k, n).astype(np.float32)
    by_word = np.ascontiguousarray(scaled.reshape(k // 512, 128, 4, n).transpose(0, 1, 3, 2))
    if fmt in ("e4m3", "e5m2"):
        words = by_word.astype(ml_dtypes.float8_e4m3fn if fmt == "e4m3" else ml_dtypes.float8_e5m2).view(np.uint8)
    else:
        c = by_word.astype(ml_dtypes.float4_e2m1fn).view(np.uint8) & 0xF
        words = (c[..., 0::2] | (c[..., 1::2] << 4)).reshape(k // 512, 128, 2 * n)
    return np.ascontiguousarray(words), np.ascontiguousarray(byte.astype(np.uint8).reshape(k // 512, 16, n))


def unpack_weight(words, scales, fmt):
    g, _, n = scales.shape
    words = np.ascontiguousarray(words).reshape(g, 128, n, -1)
    if fmt in ("e4m3", "e5m2"):
        vals = words.view(ml_dtypes.float8_e4m3fn if fmt == "e4m3" else ml_dtypes.float8_e5m2).astype(np.float64)
    else:
        nib = np.empty((g, 128, n, 4), np.uint8)
        nib[..., 0::2] = words & 0xF
        nib[..., 1::2] = words >> 4
        vals = E2M1[nib]
    vals = vals * np.repeat(np.exp2(scales.astype(np.float64) - 127.0), 8, axis=1)[..., None]
    return vals.transpose(0, 1, 3, 2).reshape(g * 512, n)


def sigmoid(v):
    return 1.0 / (1.0 + np.exp(-v))


K, T, J, R, C, O, N, E = 512, 1024, 256, 512, 512, 128, 256, 512


def setup_inputs():
    n = np.random.standard_normal
    idx = np.random.permutation(T)[:J]
    idx2 = np.random.permutation(C)[:J]
    idx3 = np.random.permutation(C)[:O]
    idx4 = np.random.permutation(C)[:O]
    idx5 = np.random.permutation(J)[:O]
    idx6 = np.random.permutation(E)[:O]
    idx7 = np.random.permutation(E)[:O]
    fk = mx_kscale(K)
    fr = mx_kscale(R)
    xtp = pack_weight(n((K, T)) / fk[:, None], "e4m3")
    wp = pack_weight(n((K, R)) * 1 / np.sqrt(K) * fk[:, None], "e2m1")
    w2p = pack_weight(n((K, R)) * 1 / np.sqrt(K) * fk[:, None], "e5m2")
    wbp = pack_weight(n((R, N)) * 1 / np.sqrt(R) / fr[:, None], "e5m2")
    return {
        "xt_words": xtp[0],
        "xt_scales": xtp[1],
        "w_words": wp[0],
        "w_scales": wp[1],
        "w2_words": w2p[0],
        "w2_scales": w2p[1],
        "sa": (np.random.uniform(0.5, 1.6, (R, 1)) * fr[:, None]).astype(np.float32),
        "sb": (np.random.uniform(0.5, 1.6, (R, 1)) * fr[:, None]).astype(np.float32),
        "bg": (np.random.uniform(-2.0, 2.0, (R, 1))).astype(np.float32),
        "wb_words": wbp[0],
        "wb_scales": wbp[1],
        "offs": striped(idx),
        "offs2": striped(idx2),
        "offs3": striped(idx3),
        "offs4": striped(idx4),
        "offs5": striped(idx5),
        "offs6": striped(idx6),
        "offs7": striped(idx7),
    }


def reference(xt_words, xt_scales, w_words, w_scales, w2_words, w2_scales, sa, sb, bg, wb_words, wb_scales, offs, offs2, offs3, offs4, offs5, offs6, offs7):
    idx = unstriped(offs)
    idx2 = unstriped(offs2)
    idx3 = unstriped(offs3)
    idx4 = unstriped(offs4)
    idx5 = unstriped(offs5)
    idx6 = unstriped(offs6)
    idx7 = unstriped(offs7)
    xtu = unpack_weight(xt_words, xt_scales, "e4m3")
    wu = unpack_weight(w_words, w_scales, "e2m1")
    w2u = unpack_weight(w2_words, w2_scales, "e5m2")
    wbu = unpack_weight(wb_words, wb_scales, "e5m2")
    xtidxg = xtu[:, idx]
    a = wu.T @ xtidxg
    b = w2u.T @ xtidxg
    lb = b[:, 0:1]
    pw = np.zeros((R, C))
    pw[:, idx2] = a
    u1 = pw[:, idx3] * f64(sa) * sigmoid(pw[:, idx4] * lb + f64(bg))
    hid = np.abs(u1 - b[:, idx5] * f64(sb))
    hidq = mxq(hid, 0, "e4m3")
    p = wbu.T @ hidq
    pa = np.zeros((N, E))
    pa[:, idx6] = p
    pb = np.zeros((N, E))
    pb[:, idx7] = p
    y = pa + pb
    return y

@@ -1,0 +1,249 @@
+from contextlib import ExitStack
+
+import concourse.mybir as mybir
+
+K, T, J, R, C, O, N, E = 512, 1024, 256, 512, 512, 128, 256, 512
+FLOPS = 2 * K * R * J * 2 + 2 * R * N * O
+
+F32 = mybir.dt.float32
+BF16 = mybir.dt.bfloat16
+I32 = mybir.dt.int32
+U32 = mybir.dt.uint32
+U16 = mybir.dt.uint16
+U8 = mybir.dt.uint8
+E4M3X4 = mybir.dt.float8_e4m3fn_x4
+E5M2X4 = mybir.dt.float8_e5m2_x4
+E2M1X4 = mybir.dt.float4_e2m1fn_x4
+ACT = mybir.ActivationFunctionType
+ALU = mybir.AluOpType
+
+P = 128
+PACK = 4
+QUADS = 4
+QROWS = 4
+LINE = 16
+
+
+def deal(copy, out, in_, per_line, first=0, last=PACK):
+    copy(
+        out=out.rearrange("p (t c i) -> p c t i", t=last - first, i=per_line),
+        in_=in_.rearrange("p (c i t) -> p c t i", t=PACK, i=per_line)[:, :, first:last, :],
+    )
+
+
+def tile_list_slopeboard_twow_one_pagetwice_kernel(
+    tc, xt_words, xt_scales, w_words, w_scales, w2_words, w2_scales, sa, sb, bg, wb_words, wb_scales,
+    offs, offs2, offs3, offs4, offs5, offs6, offs7, out,
+):
+    nc = tc.nc
+    with ExitStack() as ctx:
+        lists = ctx.enter_context(tc.tile_pool(name="lists", bufs=1))
+        keep = ctx.enter_context(tc.tile_pool(name="keep", bufs=1))
+        psum = ctx.enter_context(tc.psum_pool(name="psum", bufs=1))
+
+        def load_list(src, name):
+            tile = lists.tile(list(src.shape), U16, name=name)
+            nc.sync.dma_start(tile[:], src)
+            return tile
+
+        def zeroed_plane(width, name):
+            plane = keep.tile([P, width], U8, name=name, align_bytes=64)
+            nc.vector.memset(plane[:].bitcast(I32), 0)
+            return plane
+
+        def load_plane(engine, plane, scales):
+            for q in range(QUADS):
+                engine.dma_start(
+                    plane[32 * q : 32 * q + QROWS, :].bitcast(I32), scales[0, QROWS * q : QROWS * (q + 1), :].bitcast(I32)
+                )
+
+        def stage_plane(engine, scales, name):
+            staged = keep.tile([QROWS, QUADS, scales.shape[2] // 4], I32, name=name)
+            engine.dma_start(staged[:], scales[0].bitcast(I32).rearrange("(q r) c -> r q c", r=QROWS))
+            return staged
+
+        def spread_plane(plane, staged):
+            for q in range(QUADS):
+                nc.vector.tensor_copy(out=plane[32 * q : 32 * q + QROWS, :].bitcast(I32), in_=staged[:, q, :])
+
+        def load_rows(src, name):
+            tile = keep.tile([P, PACK], F32, name=name)
+            nc.gpsimd.dma_start(tile[:], src.rearrange("(p t) one -> p (t one)", t=PACK))
+            return tile
+
+        xt_plane = zeroed_plane(T, "xt_plane")
+        w_plane = zeroed_plane(R, "w_plane")
+        w2_plane = zeroed_plane(R, "w2_plane")
+
+        boards = [keep.tile([P, C], F32, name="board%d" % t) for t in range(PACK)]
+        for board in boards:
+            nc.vector.memset(board[:].bitcast(I32), 0)
+        wb_plane = zeroed_plane(N, "wb_plane")
+
+        tokens = load_list(offs, "tokens")
+        xt_staged = stage_plane(nc.scalar, xt_scales, "xt_staged")
+        xt_table = keep.tile([P, T], U32, name="xt_table")
+        nc.sync.dma_start(xt_table[:].bitcast(I32), xt_words[0].rearrange("p n t -> p (n t)").bitcast(I32))
+        w_staged = stage_plane(nc.scalar, w_scales, "w_staged")
+        w_raw = keep.tile([P, R], U16, name="w_raw")
+        nc.sync.dma_start(w_raw[:].bitcast(I32), w_words[0].bitcast(I32))
+        w2_staged = stage_plane(nc.scalar, w2_scales, "w2_staged")
+        w2_raw = keep.tile([P, R], U32, name="w2_raw", tag="w2_raw_then_a1")
+        nc.sync.dma_start(w2_raw[:].bitcast(I32), w2_words[0].rearrange("p n t -> p (n t)").bitcast(I32))
+        board_put = load_list(offs2, "board_put")
+        gate_pick = load_list(offs4, "gate_pick")
+        bg_rows = load_rows(bg, "bg_rows")
+        board_pick = load_list(offs3, "board_pick")
+        sa_rows = load_rows(sa, "sa_rows")
+        slot_pick = load_list(offs5, "slot_pick")
+        sb_rows = load_rows(sb, "sb_rows")
+        wb_codes = keep.tile([P, N], U32, name="wb_codes", align_bytes=64)
+        nc.sync.dma_start(wb_codes[:].bitcast(I32), wb_words[0].rearrange("p n t -> p (n t)").bitcast(I32))
+        page_puts = [load_list(offs6, "page_put_a"), load_list(offs7, "page_put_b")]
+
+        spread_plane(xt_plane, xt_staged)
+        spread_plane(w_plane, w_staged)
+        x_scales = keep.tile([P, J], U8, name="x_scales", align_bytes=64)
+        nc.vector.tensor_copy(x_scales[:], xt_plane[:].indirect(tokens[:]))
+        w_dealt_scales = keep.tile([P, R], U8, name="w_dealt_scales", align_bytes=64)
+        deal(nc.vector.tensor_copy, w_dealt_scales[:], w_plane[:], LINE)
+        x_codes = keep.tile([P, J], U32, name="x_codes", tag="page00", align_bytes=64)
+        nc.vector.tensor_copy(x_codes[:], xt_table[:].indirect(tokens[:]))
+        w_codes = keep.tile([P, R], U16, name="w_codes", tag="page01", align_bytes=64)
+        deal(nc.scalar.copy, w_codes[:], w_raw[:], LINE // 2)
+        w2_first = keep.tile([P, P], U32, name="w2_first", align_bytes=64)
+        deal(nc.scalar.copy, w2_first[:], w2_raw[:], LINE // 4, 0, 1)
+        w2_rest = keep.tile([P, R - P], U32, name="w2_rest", tag="page10", align_bytes=64)
+        deal(nc.scalar.copy, w2_rest[:], w2_raw[:], LINE // 4, 1, PACK)
+        w2_codes = [w2_first[:]] + [w2_rest[:, P * t : P * (t + 1)] for t in range(PACK - 1)]
+        spread_plane(w2_plane, w2_staged)
+        w2_dealt_scales = keep.tile([P, R], U8, name="w2_dealt_scales", tag="page11", align_bytes=64)
+        deal(nc.vector.tensor_copy, w2_dealt_scales[:], w2_plane[:], LINE)
+
+        load_plane(nc.sync, wb_plane, wb_scales)
+
+        def first_stage(codes, scales, dtype, t, bank):
+            acc = psum.tile([P, J], F32, name="acc", tag="bank%d" % bank)
+            nc.tensor.matmul_mx(
+                out=acc[:], lhsT=codes.bitcast(dtype), lhsT_scale=scales[:, P * t : P * (t + 1)],
+                rhs=x_codes[:].bitcast(E4M3X4), rhs_scale=x_scales[:], start=True, stop=True,
+            )
+            return acc
+
+        def product_a(t, bank):
+            return first_stage(w_codes[:, P * t : P * (t + 1)], w_dealt_scales, E2M1X4, t, bank)
+
+        def product_b(t, bank):
+            return first_stage(w2_codes[t], w2_dealt_scales, E5M2X4, t, bank)
+
+        a_rows = [
+            keep.tile([P, J], F32, name="a%d" % t, tag="w2_raw_then_a1" if t == 1 else "a%d" % t) for t in range(PACK)
+        ]
+        b_rows = [keep.tile([P, J], F32, name="b%d" % t) for t in range(PACK)]
+        picked = {}
+        gates = {}
+        beside = [keep.tile([P, 2 * O], F32, name="beside%d" % h) for h in range(2)]
+        gated = [keep.tile([P, 2 * O], F32, name="gated%d" % h) for h in range(2)]
+        diff = [keep.tile([P, 2 * O], F32, name="diff%d" % h) for h in range(2)]
+        hid = keep.tile([P, O, PACK], BF16, name="hid", align_bytes=64)
+
+        def part(tiles, t):
+            return tiles[t // 2][:, O * (t % 2) : O * (t % 2 + 1)]
+
+        def fetch_gate(t):
+            gates[t] = keep.tile([P, O], F32, name="gates%d" % t, tag="board%d" % (t - 1) if t else "gates0")
+            nc.scalar.activation(
+                out=gates[t][:], in_=boards[t][:].indirect(gate_pick[:]), func=ACT.Sigmoid,
+                bias=bg_rows[:, t : t + 1], scale=b_rows[t][:, 0:1],
+            )
+
+        def fetch_board(t):
+            picked[t] = keep.tile([P, O], F32, name="picked%d" % t, tag="b%d" % (t - 1) if t else "picked0")
+            nc.scalar.activation(
+                out=picked[t][:], in_=boards[t][:].indirect(board_pick[:]), func=ACT.Copy, scale=sa_rows[:, t : t + 1]
+            )
+
+        def fetch_beside(t):
+            nc.scalar.activation(
+                out=part(beside, t), in_=b_rows[t][:].indirect(slot_pick[:]), func=ACT.Copy, scale=sb_rows[:, t : t + 1]
+            )
+
+        def magnitude(h):
+            pair = diff[h][:].rearrange("p (t o) -> p o t", t=2)
+            nc.vector.scalar_tensor_tensor(
+                out=hid[:, :, 2 * h : 2 * h + 2], in0=pair, scalar=-1.0, in1=pair, op0=ALU.mult, op1=ALU.max
+            )
+
+        a0, b0, a1, b1 = product_a(0, 0), product_b(0, 1), product_a(1, 2), product_b(1, 3)
+        nc.vector.tensor_copy(a_rows[0][:], a0[:])
+        nc.vector.tensor_copy(boards[0][:].indirect(board_put[:]), a_rows[0][:])
+        nc.scalar.copy(b_rows[0][:], b0[:])
+        nc.scalar.copy(a_rows[1][:], a1[:])
+        nc.scalar.activation(out=boards[1][:].indirect(board_put[:]), in_=a_rows[1][:], func=ACT.Copy)
+        nc.vector.tensor_copy(b_rows[1][:], b1[:])
+        a2, a3, b2, b3 = product_a(2, 1), product_a(3, 3), product_b(2, 4), product_b(3, 5)
+        nc.vector.tensor_copy(a_rows[2][:], a2[:])
+        nc.vector.tensor_copy(boards[2][:].indirect(board_put[:]), a_rows[2][:])
+        nc.vector.tensor_copy(a_rows[3][:], a3[:])
+        nc.vector.tensor_copy(boards[3][:].indirect(board_put[:]), a_rows[3][:])
+        late_b = {2: b2, 3: b3}
+        for t in range(PACK):
+            if t in late_b:
+                nc.scalar.copy(b_rows[t][:], late_b[t][:])
+            fetch_beside(t)
+            fetch_gate(t)
+            fetch_board(t)
+
+        for t in range(PACK - 1):
+            nc.vector.tensor_tensor(part(gated, t), picked[t][:], gates[t][:], ALU.mult)
+        nc.vector.tensor_tensor(diff[0][:], gated[0][:], beside[0][:], ALU.subtract)
+        nc.vector.tensor_tensor(part(diff, 2), part(gated, 2), part(beside, 2), ALU.subtract)
+        nc.scalar.activation(out=hid[:, :, 0:2], in_=diff[0][:].rearrange("p (t o) -> p o t", t=2), func=ACT.Abs)
+        nc.vector.tensor_tensor(part(gated, 3), picked[3][:], gates[3][:], ALU.mult)
+        nc.vector.tensor_tensor(part(diff, 3), part(gated, 3), part(beside, 3), ALU.subtract)
+        magnitude(1)
+
+        hid_codes = keep.tile([P, O], U32, name="hid_codes", align_bytes=64)
+        hid_scales = keep.tile([P, O], U8, name="hid_scales", align_bytes=64)
+        nc.vector.quantize_mx(
+            out=hid_codes[:].bitcast(E4M3X4), scales=hid_scales[:], in_=hid[:].rearrange("p o t -> p (o t)")
+        )
+
+        halves = N // P
+        pages = [[keep.tile([P, E], F32, name="page%d%d" % (h, s), align_bytes=64) for s in range(2)] for h in range(halves)]
+        for h in range(halves):
+            for s in range(2):
+                nc.gpsimd.memset(pages[h][s][:], 0.0)
+
+        p_rows = []
+        for h in range(halves):
+            acc = psum.tile([P, O], F32, name="p_acc%d" % h, tag="bank%d" % (6 + h))
+            cols = slice(P * h, P * (h + 1))
+            nc.tensor.matmul_mx(
+                out=acc[:], lhsT=wb_codes[:, cols].bitcast(E5M2X4), lhsT_scale=wb_plane[:, cols],
+                rhs=hid_codes[:].bitcast(E4M3X4), rhs_scale=hid_scales[:], start=True, stop=True,
+            )
+            rows = keep.tile([P, O], F32, name="p%d" % h)
+            if h == 0:
+                nc.scalar.copy(rows[:], acc[:])
+            else:
+                nc.vector.tensor_copy(rows[:], acc[:])
+            p_rows.append(rows)
+
+        def add_and_store(h):
+            for s in range(2):
+                cols = slice(s * E // 2, (s + 1) * E // 2)
+                total = keep.tile([P, E // 2], F32, name="total%d%d" % (h, s))
+                nc.vector.tensor_tensor(total[:], pages[h][0][:, cols], pages[h][1][:, cols], ALU.add)
+                nc.sync.dma_start(out[P * h : P * (h + 1), cols], total[:])
+
+        half = O // 2
+        nc.vector.tensor_copy(pages[0][0][:].indirect(page_puts[0][:]), p_rows[0][:])
+        nc.scalar.activation(out=pages[0][1][:].indirect(page_puts[1][:]), in_=p_rows[0][:], func=ACT.Copy)
+        nc.scalar.activation(
+            out=pages[1][0][:].indirect(page_puts[0][:, half // 16 :]), in_=p_rows[1][:, half:], func=ACT.Copy
+        )
+        nc.scalar.activation(out=pages[1][1][:].indirect(page_puts[1][:]), in_=p_rows[1][:], func=ACT.Copy)
+        add_and_store(0)
+        nc.vector.tensor_copy(pages[1][0][:].indirect(page_puts[0][:, : half // 16]), p_rows[1][:, :half])
+        add_and_store(1)

@@ -88,6 +88,9 @@ def tile_list_slopeboard_twow_one_pagetwice_kernel(
         w_raw = keep.tile([P, R], U16, name="w_raw")
         nc.sync.dma_start(w_raw[:].bitcast(I32), w_words[0].bitcast(I32))
         w2_staged = stage_plane(nc.scalar, w2_scales, "w2_staged")
+        warm = keep.tile([P, 2], F32, name="warm")
+        nc.gpsimd.memset(warm[:, 0:1], 0.0)
+        nc.scalar.activation(out=warm[:, 1:2], in_=warm[:, 0:1], func=ACT.Sigmoid)
         w2_raw = keep.tile([P, R], U32, name="w2_raw", tag="w2_raw_then_a1")
         nc.sync.dma_start(w2_raw[:].bitcast(I32), w2_words[0].rearrange("p n t -> p (n t)").bitcast(I32))
         board_put = load_list(offs2, "board_put")

@@ -68,7 +68,7 @@ def tile_list_slopeboard_twow_one_pagetwice_kernel(
 
         def load_rows(src, name):
             tile = keep.tile([P, PACK], F32, name=name)
-            nc.gpsimd.dma_start(tile[:], src.rearrange("(p t) one -> p (t one)", t=PACK))
+            nc.sync.dma_start(tile[:], src.rearrange("(p t) one -> p (t one)", t=PACK))
             return tile
 
         xt_plane = zeroed_plane(T, "xt_plane")
@@ -76,22 +76,22 @@ def tile_list_slopeboard_twow_one_pagetwice_kernel(
         w2_plane = zeroed_plane(R, "w2_plane")
 
         boards = [keep.tile([P, C], F32, name="board%d" % t) for t in range(PACK)]
-        for board in boards:
-            nc.vector.memset(board[:].bitcast(I32), 0)
+        for t, board in enumerate(boards):
+            (nc.vector if t < 2 else nc.gpsimd).memset(board[:].bitcast(I32), 0)
         wb_plane = zeroed_plane(N, "wb_plane")
 
         tokens = load_list(offs, "tokens")
         xt_staged = stage_plane(nc.scalar, xt_scales, "xt_staged")
-        xt_table = keep.tile([P, T], U32, name="xt_table")
-        nc.sync.dma_start(xt_table[:].bitcast(I32), xt_words[0].rearrange("p n t -> p (n t)").bitcast(I32))
-        w_staged = stage_plane(nc.scalar, w_scales, "w_staged")
         w_raw = keep.tile([P, R], U16, name="w_raw")
         nc.sync.dma_start(w_raw[:].bitcast(I32), w_words[0].bitcast(I32))
-        w2_staged = stage_plane(nc.scalar, w2_scales, "w2_staged")
+        w_staged = stage_plane(nc.scalar, w_scales, "w_staged")
+        xt_table = keep.tile([P, T], U32, name="xt_table")
+        nc.sync.dma_start(xt_table[:].bitcast(I32), xt_words[0].rearrange("p n t -> p (n t)").bitcast(I32))
         warm = keep.tile([P, 2], F32, name="warm")
         nc.gpsimd.memset(warm[:, 0:1], 0.0)
         nc.scalar.activation(out=warm[:, 1:2], in_=warm[:, 0:1], func=ACT.Sigmoid)
-        w2_raw = keep.tile([P, R], U32, name="w2_raw", tag="w2_raw_then_a1")
+        w2_staged = stage_plane(nc.sync, w2_scales, "w2_staged")
+        w2_raw = keep.tile([P, R], U32, name="w2_raw")
         nc.sync.dma_start(w2_raw[:].bitcast(I32), w2_words[0].rearrange("p n t -> p (n t)").bitcast(I32))
         board_put = load_list(offs2, "board_put")
         gate_pick = load_list(offs4, "gate_pick")
@@ -121,7 +121,7 @@ def tile_list_slopeboard_twow_one_pagetwice_kernel(
         w2_codes = [w2_first[:]] + [w2_rest[:, P * t : P * (t + 1)] for t in range(PACK - 1)]
         spread_plane(w2_plane, w2_staged)
         w2_dealt_scales = keep.tile([P, R], U8, name="w2_dealt_scales", tag="page11", align_bytes=64)
-        deal(nc.vector.tensor_copy, w2_dealt_scales[:], w2_plane[:], LINE)
+        deal(nc.gpsimd.tensor_copy, w2_dealt_scales[:], w2_plane[:], LINE)
 
         load_plane(nc.sync, wb_plane, wb_scales)
 
@@ -139,9 +139,7 @@ def tile_list_slopeboard_twow_one_pagetwice_kernel(
         def product_b(t, bank):
             return first_stage(w2_codes[t], w2_dealt_scales, E5M2X4, t, bank)
 
-        a_rows = [
-            keep.tile([P, J], F32, name="a%d" % t, tag="w2_raw_then_a1" if t == 1 else "a%d" % t) for t in range(PACK)
-        ]
+        a_rows = [keep.tile([P, J], F32, name="a%d" % t) for t in range(PACK)]
         b_rows = [keep.tile([P, J], F32, name="b%d" % t) for t in range(PACK)]
         picked = {}
         gates = {}
@@ -172,27 +170,21 @@ def tile_list_slopeboard_twow_one_pagetwice_kernel(
             )
 
         def magnitude(h):
-            pair = diff[h][:].rearrange("p (t o) -> p o t", t=2)
-            nc.vector.scalar_tensor_tensor(
-                out=hid[:, :, 2 * h : 2 * h + 2], in0=pair, scalar=-1.0, in1=pair, op0=ALU.mult, op1=ALU.max
+            nc.scalar.activation(
+                out=hid[:, :, 2 * h : 2 * h + 2], in_=diff[h][:].rearrange("p (t o) -> p o t", t=2), func=ACT.Abs
             )
 
-        a0, b0, a1, b1 = product_a(0, 0), product_b(0, 1), product_a(1, 2), product_b(1, 3)
-        nc.vector.tensor_copy(a_rows[0][:], a0[:])
-        nc.vector.tensor_copy(boards[0][:].indirect(board_put[:]), a_rows[0][:])
-        nc.scalar.copy(b_rows[0][:], b0[:])
-        nc.scalar.copy(a_rows[1][:], a1[:])
-        nc.scalar.activation(out=boards[1][:].indirect(board_put[:]), in_=a_rows[1][:], func=ACT.Copy)
-        nc.vector.tensor_copy(b_rows[1][:], b1[:])
-        a2, a3, b2, b3 = product_a(2, 1), product_a(3, 3), product_b(2, 4), product_b(3, 5)
-        nc.vector.tensor_copy(a_rows[2][:], a2[:])
-        nc.vector.tensor_copy(boards[2][:].indirect(board_put[:]), a_rows[2][:])
-        nc.vector.tensor_copy(a_rows[3][:], a3[:])
-        nc.vector.tensor_copy(boards[3][:].indirect(board_put[:]), a_rows[3][:])
-        late_b = {2: b2, 3: b3}
+        a_acc = [product_a(t, t) for t in range(PACK)]
+        b_acc = [product_b(t, PACK + t) for t in range(PACK)]
+        nc.vector.tensor_copy(a_rows[0][:], a_acc[0][:])
+        nc.scalar.activation(out=boards[0][:].indirect(board_put[:]), in_=a_rows[0][:], func=ACT.Copy)
+        nc.vector.tensor_copy(a_rows[1][:], a_acc[1][:])
+        for t in range(1, PACK):
+            if t + 1 < PACK:
+                nc.vector.tensor_copy(a_rows[t + 1][:], a_acc[t + 1][:])
+            nc.vector.tensor_copy(boards[t][:].indirect(board_put[:]), a_rows[t][:])
         for t in range(PACK):
-            if t in late_b:
-                nc.scalar.copy(b_rows[t][:], late_b[t][:])
+            nc.scalar.copy(b_rows[t][:], b_acc[t][:])
             fetch_beside(t)
             fetch_gate(t)
             fetch_board(t)
@@ -201,7 +193,7 @@ def tile_list_slopeboard_twow_one_pagetwice_kernel(
             nc.vector.tensor_tensor(part(gated, t), picked[t][:], gates[t][:], ALU.mult)
         nc.vector.tensor_tensor(diff[0][:], gated[0][:], beside[0][:], ALU.subtract)
         nc.vector.tensor_tensor(part(diff, 2), part(gated, 2), part(beside, 2), ALU.subtract)
-        nc.scalar.activation(out=hid[:, :, 0:2], in_=diff[0][:].rearrange("p (t o) -> p o t", t=2), func=ACT.Abs)
+        magnitude(0)
         nc.vector.tensor_tensor(part(gated, 3), picked[3][:], gates[3][:], ALU.mult)
         nc.vector.tensor_tensor(part(diff, 3), part(gated, 3), part(beside, 3), ALU.subtract)
         magnitude(1)
@@ -220,7 +212,7 @@ def tile_list_slopeboard_twow_one_pagetwice_kernel(
 
         p_rows = []
         for h in range(halves):
-            acc = psum.tile([P, O], F32, name="p_acc%d" % h, tag="bank%d" % (6 + h))
+            acc = psum.tile([P, O], F32, name="p_acc%d" % h, tag="bank%d" % h)
             cols = slice(P * h, P * (h + 1))
             nc.tensor.matmul_mx(
                 out=acc[:], lhsT=wb_codes[:, cols].bitcast(E5M2X4), lhsT_scale=wb_plane[:, cols],
@@ -233,20 +225,13 @@ def tile_list_slopeboard_twow_one_pagetwice_kernel(
                 nc.vector.tensor_copy(rows[:], acc[:])
             p_rows.append(rows)
 
-        def add_and_store(h):
+        for h in range(halves):
+            nc.vector.tensor_copy(pages[h][0][:].indirect(page_puts[0][:]), p_rows[h][:])
+            nc.scalar.activation(out=pages[h][1][:].indirect(page_puts[1][:]), in_=p_rows[h][:], func=ACT.Copy)
+        for h in range(halves):
             for s in range(2):
                 cols = slice(s * E // 2, (s + 1) * E // 2)
                 total = keep.tile([P, E // 2], F32, name="total%d%d" % (h, s))
-                nc.vector.tensor_tensor(total[:], pages[h][0][:, cols], pages[h][1][:, cols], ALU.add)
+                engine = nc.gpsimd if (h, s) == (0, 0) else nc.vector
+                engine.tensor_tensor(total[:], pages[h][0][:, cols], pages[h][1][:, cols], ALU.add)
                 nc.sync.dma_start(out[P * h : P * (h + 1), cols], total[:])
-
-        half = O // 2
-        nc.vector.tensor_copy(pages[0][0][:].indirect(page_puts[0][:]), p_rows[0][:])
-        nc.scalar.activation(out=pages[0][1][:].indirect(page_puts[1][:]), in_=p_rows[0][:], func=ACT.Copy)
-        nc.scalar.activation(
-            out=pages[1][0][:].indirect(page_puts[0][:, half // 16 :]), in_=p_rows[1][:, half:], func=ACT.Copy
-        )
-        nc.scalar.activation(out=pages[1][1][:].indirect(page_puts[1][:]), in_=p_rows[1][:], func=ACT.Copy)
-        add_and_store(0)
-        nc.vector.tensor_copy(pages[1][0][:].indirect(page_puts[0][:, : half // 16]), p_rows[1][:, :half])
-        add_and_store(1)

@@ -109,7 +109,7 @@ def tile_list_slopeboard_twow_one_pagetwice_kernel(
         x_scales = keep.tile([P, J], U8, name="x_scales", align_bytes=64)
         nc.vector.tensor_copy(x_scales[:], xt_plane[:].indirect(tokens[:]))
         w_dealt_scales = keep.tile([P, R], U8, name="w_dealt_scales", align_bytes=64)
-        deal(nc.vector.tensor_copy, w_dealt_scales[:], w_plane[:], LINE)
+        deal(nc.gpsimd.tensor_copy, w_dealt_scales[:], w_plane[:], LINE)
         x_codes = keep.tile([P, J], U32, name="x_codes", tag="page00", align_bytes=64)
         nc.vector.tensor_copy(x_codes[:], xt_table[:].indirect(tokens[:]))
         w_codes = keep.tile([P, R], U16, name="w_codes", tag="page01", align_bytes=64)
@@ -166,7 +166,7 @@ def tile_list_slopeboard_twow_one_pagetwice_kernel(
 
         def fetch_beside(t):
             nc.scalar.activation(
-                out=part(beside, t), in_=b_rows[t][:].indirect(slot_pick[:]), func=ACT.Copy, scale=sb_rows[:, t : t + 1]
+                out=beside_last[:] if t == PACK - 1 else part(beside, t), in_=b_rows[t][:].indirect(slot_pick[:]), func=ACT.Copy, scale=sb_rows[:, t : t + 1]
             )
 
         def magnitude(h):
@@ -183,19 +183,32 @@ def tile_list_slopeboard_twow_one_pagetwice_kernel(
             if t + 1 < PACK:
                 nc.vector.tensor_copy(a_rows[t + 1][:], a_acc[t + 1][:])
             nc.vector.tensor_copy(boards[t][:].indirect(board_put[:]), a_rows[t][:])
-        for t in range(PACK):
+        last = PACK - 1
+        nc.vector.tensor_copy(b_rows[last][:], b_acc[last][:])
+        for t in range(last):
             nc.scalar.copy(b_rows[t][:], b_acc[t][:])
             fetch_beside(t)
             fetch_gate(t)
             fetch_board(t)
+        fetch_board(last)
+        fetch_gate(last)
+        beside_last = keep.tile([P, O], F32, name="beside_last", tag="board%d" % last)
+        fetch_beside(last)
 
-        for t in range(PACK - 1):
+        halves = N // P
+        pages = [[keep.tile([P, E], F32, name="page%d%d" % (h, s), align_bytes=64) for s in range(2)] for h in range(halves)]
+        for h in range(halves):
+            for s in range(2):
+                nc.gpsimd.memset(pages[h][s][:], 0.0)
+
+        for t in range(2):
+            nc.gpsimd.tensor_tensor(part(gated, t), picked[t][:], gates[t][:], ALU.mult)
+        nc.gpsimd.tensor_tensor(diff[0][:], gated[0][:], beside[0][:], ALU.subtract)
+        pair = diff[0][:].rearrange("p (t o) -> p o t", t=2)
+        nc.vector.scalar_tensor_tensor(out=hid[:, :, 0:2], in0=pair, scalar=-1.0, in1=pair, op0=ALU.mult, op1=ALU.max)
+        for t in range(2, PACK):
             nc.vector.tensor_tensor(part(gated, t), picked[t][:], gates[t][:], ALU.mult)
-        nc.vector.tensor_tensor(diff[0][:], gated[0][:], beside[0][:], ALU.subtract)
-        nc.vector.tensor_tensor(part(diff, 2), part(gated, 2), part(beside, 2), ALU.subtract)
-        magnitude(0)
-        nc.vector.tensor_tensor(part(gated, 3), picked[3][:], gates[3][:], ALU.mult)
-        nc.vector.tensor_tensor(part(diff, 3), part(gated, 3), part(beside, 3), ALU.subtract)
+            nc.vector.tensor_tensor(part(diff, t), part(gated, t), beside_last[:] if t == last else part(beside, t), ALU.subtract)
         magnitude(1)
 
         hid_codes = keep.tile([P, O], U32, name="hid_codes", align_bytes=64)
@@ -203,12 +216,6 @@ def tile_list_slopeboard_twow_one_pagetwice_kernel(
         nc.vector.quantize_mx(
             out=hid_codes[:].bitcast(E4M3X4), scales=hid_scales[:], in_=hid[:].rearrange("p o t -> p (o t)")
         )
-
-        halves = N // P
-        pages = [[keep.tile([P, E], F32, name="page%d%d" % (h, s), align_bytes=64) for s in range(2)] for h in range(halves)]
-        for h in range(halves):
-            for s in range(2):
-                nc.gpsimd.memset(pages[h][s][:], 0.0)
 
         p_rows = []
         for h in range(halves):
@@ -234,4 +241,5 @@ def tile_list_slopeboard_twow_one_pagetwice_kernel(
                 total = keep.tile([P, E // 2], F32, name="total%d%d" % (h, s))
                 engine = nc.gpsimd if (h, s) == (0, 0) else nc.vector
                 engine.tensor_tensor(total[:], pages[h][0][:, cols], pages[h][1][:, cols], ALU.add)
-                nc.sync.dma_start(out[P * h : P * (h + 1), cols], total[:])
+                queue = nc.scalar if (h, s) == (0, 0) else nc.sync
+                queue.dma_start(out[P * h : P * (h + 1), cols], total[:])

@@ -18,16 +18,20 @@ ACT = mybir.ActivationFunctionType
 ALU = mybir.AluOpType
 
 P = 128
-PACK = 4
+SETS = 4
+LAST = SETS - 1
 QUADS = 4
+QUAD = P // QUADS
 QROWS = 4
-LINE = 16
+RUN_BYTES = 16
+HALVES = N // P
+BOARDS_ON_VECTOR = 2
 
 
-def deal(copy, out, in_, per_line, first=0, last=PACK):
+def deal(copy, out, in_, run, first=0, stop=SETS):
     copy(
-        out=out.rearrange("p (t c i) -> p c t i", t=last - first, i=per_line),
-        in_=in_.rearrange("p (c i t) -> p c t i", t=PACK, i=per_line)[:, :, first:last, :],
+        out=out.rearrange("p (t c i) -> p c t i", t=stop - first, i=run),
+        in_=in_.rearrange("p (c i t) -> p c t i", t=SETS, i=run)[:, :, first:stop, :],
     )
 
 
@@ -46,110 +50,105 @@ def tile_list_slopeboard_twow_one_pagetwice_kernel(
             nc.sync.dma_start(tile[:], src)
             return tile
 
+        def load_fp8_words(tile, words):
+            nc.sync.dma_start(tile[:].bitcast(I32), words[0].rearrange("p n i -> p (n i)").bitcast(I32))
+
+        def load_row_values(src, name):
+            tile = keep.tile([P, SETS], F32, name=name)
+            nc.sync.dma_start(tile[:], src.rearrange("(p t) one -> p (t one)", t=SETS))
+            return tile
+
         def zeroed_plane(width, name):
             plane = keep.tile([P, width], U8, name=name, align_bytes=64)
             nc.vector.memset(plane[:].bitcast(I32), 0)
             return plane
 
-        def load_plane(engine, plane, scales):
-            for q in range(QUADS):
-                engine.dma_start(
-                    plane[32 * q : 32 * q + QROWS, :].bitcast(I32), scales[0, QROWS * q : QROWS * (q + 1), :].bitcast(I32)
-                )
+        def live_rows(plane, q):
+            return plane[QUAD * q : QUAD * q + QROWS, :].bitcast(I32)
 
-        def stage_plane(engine, scales, name):
+        def stage_scales(queue, scales, name):
             staged = keep.tile([QROWS, QUADS, scales.shape[2] // 4], I32, name=name)
-            engine.dma_start(staged[:], scales[0].bitcast(I32).rearrange("(q r) c -> r q c", r=QROWS))
+            queue.dma_start(staged[:], scales[0].bitcast(I32).rearrange("(q s) c -> s q c", s=QROWS))
             return staged
 
-        def spread_plane(plane, staged):
+        def spread_scales(plane, staged):
             for q in range(QUADS):
-                nc.vector.tensor_copy(out=plane[32 * q : 32 * q + QROWS, :].bitcast(I32), in_=staged[:, q, :])
-
-        def load_rows(src, name):
-            tile = keep.tile([P, PACK], F32, name=name)
-            nc.sync.dma_start(tile[:], src.rearrange("(p t) one -> p (t one)", t=PACK))
-            return tile
+                nc.vector.tensor_copy(out=live_rows(plane, q), in_=staged[:, q, :])
 
         xt_plane = zeroed_plane(T, "xt_plane")
         w_plane = zeroed_plane(R, "w_plane")
         w2_plane = zeroed_plane(R, "w2_plane")
-
-        boards = [keep.tile([P, C], F32, name="board%d" % t) for t in range(PACK)]
+        boards = [keep.tile([P, C], F32, name="board%d" % t) for t in range(SETS)]
         for t, board in enumerate(boards):
-            (nc.vector if t < 2 else nc.gpsimd).memset(board[:].bitcast(I32), 0)
+            (nc.vector if t < BOARDS_ON_VECTOR else nc.gpsimd).memset(board[:].bitcast(I32), 0)
         wb_plane = zeroed_plane(N, "wb_plane")
 
         tokens = load_list(offs, "tokens")
-        xt_staged = stage_plane(nc.scalar, xt_scales, "xt_staged")
+        xt_staged = stage_scales(nc.scalar, xt_scales, "xt_staged")
         w_raw = keep.tile([P, R], U16, name="w_raw")
         nc.sync.dma_start(w_raw[:].bitcast(I32), w_words[0].bitcast(I32))
-        w_staged = stage_plane(nc.scalar, w_scales, "w_staged")
+        w_staged = stage_scales(nc.scalar, w_scales, "w_staged")
         xt_table = keep.tile([P, T], U32, name="xt_table")
-        nc.sync.dma_start(xt_table[:].bitcast(I32), xt_words[0].rearrange("p n t -> p (n t)").bitcast(I32))
+        load_fp8_words(xt_table, xt_words)
+
         warm = keep.tile([P, 2], F32, name="warm")
         nc.gpsimd.memset(warm[:, 0:1], 0.0)
         nc.scalar.activation(out=warm[:, 1:2], in_=warm[:, 0:1], func=ACT.Sigmoid)
-        w2_staged = stage_plane(nc.sync, w2_scales, "w2_staged")
+
+        w2_staged = stage_scales(nc.sync, w2_scales, "w2_staged")
         w2_raw = keep.tile([P, R], U32, name="w2_raw")
-        nc.sync.dma_start(w2_raw[:].bitcast(I32), w2_words[0].rearrange("p n t -> p (n t)").bitcast(I32))
+        load_fp8_words(w2_raw, w2_words)
         board_put = load_list(offs2, "board_put")
         gate_pick = load_list(offs4, "gate_pick")
-        bg_rows = load_rows(bg, "bg_rows")
+        bg_rows = load_row_values(bg, "bg_rows")
         board_pick = load_list(offs3, "board_pick")
-        sa_rows = load_rows(sa, "sa_rows")
+        sa_rows = load_row_values(sa, "sa_rows")
         slot_pick = load_list(offs5, "slot_pick")
-        sb_rows = load_rows(sb, "sb_rows")
+        sb_rows = load_row_values(sb, "sb_rows")
         wb_codes = keep.tile([P, N], U32, name="wb_codes", align_bytes=64)
-        nc.sync.dma_start(wb_codes[:].bitcast(I32), wb_words[0].rearrange("p n t -> p (n t)").bitcast(I32))
+        load_fp8_words(wb_codes, wb_words)
         page_puts = [load_list(offs6, "page_put_a"), load_list(offs7, "page_put_b")]
 
-        spread_plane(xt_plane, xt_staged)
-        spread_plane(w_plane, w_staged)
+        spread_scales(xt_plane, xt_staged)
+        spread_scales(w_plane, w_staged)
         x_scales = keep.tile([P, J], U8, name="x_scales", align_bytes=64)
         nc.vector.tensor_copy(x_scales[:], xt_plane[:].indirect(tokens[:]))
         w_dealt_scales = keep.tile([P, R], U8, name="w_dealt_scales", align_bytes=64)
-        deal(nc.gpsimd.tensor_copy, w_dealt_scales[:], w_plane[:], LINE)
+        deal(nc.vector.tensor_copy, w_dealt_scales[:], w_plane[:], RUN_BYTES)
         x_codes = keep.tile([P, J], U32, name="x_codes", tag="page00", align_bytes=64)
         nc.vector.tensor_copy(x_codes[:], xt_table[:].indirect(tokens[:]))
         w_codes = keep.tile([P, R], U16, name="w_codes", tag="page01", align_bytes=64)
-        deal(nc.scalar.copy, w_codes[:], w_raw[:], LINE // 2)
+        deal(nc.scalar.copy, w_codes[:], w_raw[:], RUN_BYTES // 2)
         w2_first = keep.tile([P, P], U32, name="w2_first", align_bytes=64)
-        deal(nc.scalar.copy, w2_first[:], w2_raw[:], LINE // 4, 0, 1)
-        w2_rest = keep.tile([P, R - P], U32, name="w2_rest", tag="page10", align_bytes=64)
-        deal(nc.scalar.copy, w2_rest[:], w2_raw[:], LINE // 4, 1, PACK)
-        w2_codes = [w2_first[:]] + [w2_rest[:, P * t : P * (t + 1)] for t in range(PACK - 1)]
-        spread_plane(w2_plane, w2_staged)
-        w2_dealt_scales = keep.tile([P, R], U8, name="w2_dealt_scales", tag="page11", align_bytes=64)
-        deal(nc.gpsimd.tensor_copy, w2_dealt_scales[:], w2_plane[:], LINE)
+        deal(nc.scalar.copy, w2_first[:], w2_raw[:], RUN_BYTES // 4, 0, 1)
+        w2_rest = keep.tile([P, R - P], U32, name="w2_rest", align_bytes=64)
+        deal(nc.scalar.copy, w2_rest[:], w2_raw[:], RUN_BYTES // 4, 1, SETS)
+        w2_codes = [w2_first[:]] + [w2_rest[:, P * t : P * (t + 1)] for t in range(SETS - 1)]
+        spread_scales(w2_plane, w2_staged)
+        w2_dealt_scales = keep.tile([P, R], U8, name="w2_dealt_scales", align_bytes=64)
+        deal(nc.gpsimd.tensor_copy, w2_dealt_scales[:], w2_plane[:], RUN_BYTES)
 
-        load_plane(nc.sync, wb_plane, wb_scales)
+        for q in range(QUADS):
+            nc.sync.dma_start(live_rows(wb_plane, q), wb_scales[0, QROWS * q : QROWS * (q + 1), :].bitcast(I32))
 
-        def first_stage(codes, scales, dtype, t, bank):
+        def first_product(codes, dealt_scales, dtype, t, bank):
             acc = psum.tile([P, J], F32, name="acc", tag="bank%d" % bank)
             nc.tensor.matmul_mx(
-                out=acc[:], lhsT=codes.bitcast(dtype), lhsT_scale=scales[:, P * t : P * (t + 1)],
+                out=acc[:], lhsT=codes.bitcast(dtype), lhsT_scale=dealt_scales[:, P * t : P * (t + 1)],
                 rhs=x_codes[:].bitcast(E4M3X4), rhs_scale=x_scales[:], start=True, stop=True,
             )
             return acc
 
-        def product_a(t, bank):
-            return first_stage(w_codes[:, P * t : P * (t + 1)], w_dealt_scales, E2M1X4, t, bank)
-
-        def product_b(t, bank):
-            return first_stage(w2_codes[t], w2_dealt_scales, E5M2X4, t, bank)
-
-        a_rows = [keep.tile([P, J], F32, name="a%d" % t) for t in range(PACK)]
-        b_rows = [keep.tile([P, J], F32, name="b%d" % t) for t in range(PACK)]
-        picked = {}
-        gates = {}
-        beside = [keep.tile([P, 2 * O], F32, name="beside%d" % h) for h in range(2)]
+        a_rows = [keep.tile([P, J], F32, name="a%d" % t) for t in range(SETS)]
+        b_rows = [keep.tile([P, J], F32, name="b%d" % t) for t in range(SETS)]
+        picked, gates, beside = {}, {}, {}
+        beside_pair0 = keep.tile([P, 2 * O], F32, name="beside_pair0")
         gated = [keep.tile([P, 2 * O], F32, name="gated%d" % h) for h in range(2)]
         diff = [keep.tile([P, 2 * O], F32, name="diff%d" % h) for h in range(2)]
-        hid = keep.tile([P, O, PACK], BF16, name="hid", align_bytes=64)
+        hid = keep.tile([P, O, SETS], BF16, name="hid", align_bytes=64)
 
-        def part(tiles, t):
-            return tiles[t // 2][:, O * (t % 2) : O * (t % 2 + 1)]
+        def in_pair(pair, t):
+            return pair[:, O * (t % 2) : O * (t % 2 + 1)]
 
         def fetch_gate(t):
             gates[t] = keep.tile([P, O], F32, name="gates%d" % t, tag="board%d" % (t - 1) if t else "gates0")
@@ -164,52 +163,53 @@ def tile_list_slopeboard_twow_one_pagetwice_kernel(
                 out=picked[t][:], in_=boards[t][:].indirect(board_pick[:]), func=ACT.Copy, scale=sa_rows[:, t : t + 1]
             )
 
-        def fetch_beside(t):
+        def fetch_beside(t, into):
+            beside[t] = into
             nc.scalar.activation(
-                out=beside_last[:] if t == PACK - 1 else part(beside, t), in_=b_rows[t][:].indirect(slot_pick[:]), func=ACT.Copy, scale=sb_rows[:, t : t + 1]
+                out=into, in_=b_rows[t][:].indirect(slot_pick[:]), func=ACT.Copy, scale=sb_rows[:, t : t + 1]
             )
 
-        def magnitude(h):
-            nc.scalar.activation(
-                out=hid[:, :, 2 * h : 2 * h + 2], in_=diff[h][:].rearrange("p (t o) -> p o t", t=2), func=ACT.Abs
-            )
+        a_acc = [first_product(w_codes[:, P * t : P * (t + 1)], w_dealt_scales, E2M1X4, t, t) for t in range(SETS)]
+        b_acc = [first_product(w2_codes[t], w2_dealt_scales, E5M2X4, t, SETS + t) for t in range(SETS)]
 
-        a_acc = [product_a(t, t) for t in range(PACK)]
-        b_acc = [product_b(t, PACK + t) for t in range(PACK)]
         nc.vector.tensor_copy(a_rows[0][:], a_acc[0][:])
         nc.scalar.activation(out=boards[0][:].indirect(board_put[:]), in_=a_rows[0][:], func=ACT.Copy)
         nc.vector.tensor_copy(a_rows[1][:], a_acc[1][:])
-        for t in range(1, PACK):
-            if t + 1 < PACK:
+        for t in range(1, SETS):
+            if t < LAST:
                 nc.vector.tensor_copy(a_rows[t + 1][:], a_acc[t + 1][:])
             nc.vector.tensor_copy(boards[t][:].indirect(board_put[:]), a_rows[t][:])
-        last = PACK - 1
-        nc.vector.tensor_copy(b_rows[last][:], b_acc[last][:])
-        for t in range(last):
-            nc.scalar.copy(b_rows[t][:], b_acc[t][:])
-            fetch_beside(t)
-            fetch_gate(t)
-            fetch_board(t)
-        fetch_board(last)
-        fetch_gate(last)
-        beside_last = keep.tile([P, O], F32, name="beside_last", tag="board%d" % last)
-        fetch_beside(last)
+        nc.vector.tensor_copy(b_rows[LAST][:], b_acc[LAST][:])
 
-        halves = N // P
-        pages = [[keep.tile([P, E], F32, name="page%d%d" % (h, s), align_bytes=64) for s in range(2)] for h in range(halves)]
-        for h in range(halves):
-            for s in range(2):
-                nc.gpsimd.memset(pages[h][s][:], 0.0)
+        fetch_board(0)
+        for t in range(LAST):
+            nc.scalar.copy(b_rows[t][:], b_acc[t][:])
+            fetch_beside(t, in_pair(beside_pair0, t) if t < 2 else keep.tile([P, O], F32, name="beside%d" % t)[:])
+            fetch_gate(t)
+            if t > 0:
+                fetch_board(t)
+        fetch_board(LAST)
+        fetch_gate(LAST)
+        fetch_beside(LAST, keep.tile([P, O], F32, name="beside%d" % LAST, tag="board%d" % LAST)[:])
+
+        pages = [
+            [keep.tile([P, E], F32, name="page0%d" % s, align_bytes=64) for s in range(2)],
+            [keep.tile([P, E], F32, name="page1%d" % s, tag="%s%d" % (rows, LAST)) for s, rows in enumerate("ab")],
+        ]
+        for half in pages:
+            for page in half:
+                nc.gpsimd.memset(page[:], 0.0)
 
         for t in range(2):
-            nc.gpsimd.tensor_tensor(part(gated, t), picked[t][:], gates[t][:], ALU.mult)
-        nc.gpsimd.tensor_tensor(diff[0][:], gated[0][:], beside[0][:], ALU.subtract)
-        pair = diff[0][:].rearrange("p (t o) -> p o t", t=2)
-        nc.vector.scalar_tensor_tensor(out=hid[:, :, 0:2], in0=pair, scalar=-1.0, in1=pair, op0=ALU.mult, op1=ALU.max)
-        for t in range(2, PACK):
-            nc.vector.tensor_tensor(part(gated, t), picked[t][:], gates[t][:], ALU.mult)
-            nc.vector.tensor_tensor(part(diff, t), part(gated, t), beside_last[:] if t == last else part(beside, t), ALU.subtract)
-        magnitude(1)
+            nc.vector.tensor_tensor(in_pair(gated[0], t), picked[t][:], gates[t][:], ALU.mult)
+        nc.vector.tensor_tensor(diff[0][:], gated[0][:], beside_pair0[:], ALU.subtract)
+        for t in range(2, SETS):
+            nc.vector.tensor_tensor(in_pair(gated[1], t), picked[t][:], gates[t][:], ALU.mult)
+            nc.vector.tensor_tensor(in_pair(diff[1], t), in_pair(gated[1], t), beside[t], ALU.subtract)
+        for h in range(2):
+            nc.scalar.activation(
+                out=hid[:, :, 2 * h : 2 * h + 2], in_=diff[h][:].rearrange("p (t o) -> p o t", t=2), func=ACT.Abs
+            )
 
         hid_codes = keep.tile([P, O], U32, name="hid_codes", align_bytes=64)
         hid_scales = keep.tile([P, O], U8, name="hid_scales", align_bytes=64)
@@ -218,28 +218,26 @@ def tile_list_slopeboard_twow_one_pagetwice_kernel(
         )
 
         p_rows = []
-        for h in range(halves):
+        for h, copy in enumerate((nc.scalar.copy, nc.vector.tensor_copy)):
             acc = psum.tile([P, O], F32, name="p_acc%d" % h, tag="bank%d" % h)
             cols = slice(P * h, P * (h + 1))
             nc.tensor.matmul_mx(
                 out=acc[:], lhsT=wb_codes[:, cols].bitcast(E5M2X4), lhsT_scale=wb_plane[:, cols],
                 rhs=hid_codes[:].bitcast(E4M3X4), rhs_scale=hid_scales[:], start=True, stop=True,
             )
-            rows = keep.tile([P, O], F32, name="p%d" % h)
-            if h == 0:
-                nc.scalar.copy(rows[:], acc[:])
-            else:
-                nc.vector.tensor_copy(rows[:], acc[:])
-            p_rows.append(rows)
+            p_rows.append(keep.tile([P, O], F32, name="p%d" % h))
+            copy(p_rows[h][:], acc[:])
 
-        for h in range(halves):
+        for h in range(HALVES):
             nc.vector.tensor_copy(pages[h][0][:].indirect(page_puts[0][:]), p_rows[h][:])
             nc.scalar.activation(out=pages[h][1][:].indirect(page_puts[1][:]), in_=p_rows[h][:], func=ACT.Copy)
-        for h in range(halves):
-            for s in range(2):
-                cols = slice(s * E // 2, (s + 1) * E // 2)
-                total = keep.tile([P, E // 2], F32, name="total%d%d" % (h, s))
-                engine = nc.gpsimd if (h, s) == (0, 0) else nc.vector
-                engine.tensor_tensor(total[:], pages[h][0][:, cols], pages[h][1][:, cols], ALU.add)
-                queue = nc.scalar if (h, s) == (0, 0) else nc.sync
+
+        for h in range(HALVES):
+            for side in range(2):
+                first_quarter = (h, side) == (0, 0)
+                cols = slice(side * E // 2, (side + 1) * E // 2)
+                total = keep.tile([P, E // 2], F32, name="total%d%d" % (h, side))
+                adder = nc.gpsimd if first_quarter else nc.vector
+                adder.tensor_tensor(total[:], pages[h][0][:, cols], pages[h][1][:, cols], ALU.add)
+                queue = nc.scalar if first_quarter else nc.sync
                 queue.dma_start(out[P * h : P * (h + 1), cols], total[:])

from contextlib import ExitStack

import concourse.mybir as mybir

K, T, J, R, C, O, N, E = 512, 1024, 256, 512, 512, 128, 256, 512
FLOPS = 2 * K * R * J * 2 + 2 * R * N * O

F32 = mybir.dt.float32
BF16 = mybir.dt.bfloat16
I32 = mybir.dt.int32
U32 = mybir.dt.uint32
U16 = mybir.dt.uint16
U8 = mybir.dt.uint8
E4M3X4 = mybir.dt.float8_e4m3fn_x4
E5M2X4 = mybir.dt.float8_e5m2_x4
E2M1X4 = mybir.dt.float4_e2m1fn_x4
ACT = mybir.ActivationFunctionType
ALU = mybir.AluOpType

P = 128
SETS = 4
LAST = SETS - 1
QUADS = 4
QUAD = P // QUADS
QROWS = 4
RUN_BYTES = 16
HALVES = N // P
BOARDS_ON_VECTOR = 2


def deal(copy, out, in_, run, first=0, stop=SETS):
    copy(
        out=out.rearrange("p (t c i) -> p c t i", t=stop - first, i=run),
        in_=in_.rearrange("p (c i t) -> p c t i", t=SETS, i=run)[:, :, first:stop, :],
    )


def tile_list_slopeboard_twow_one_pagetwice_kernel(
    tc, xt_words, xt_scales, w_words, w_scales, w2_words, w2_scales, sa, sb, bg, wb_words, wb_scales,
    offs, offs2, offs3, offs4, offs5, offs6, offs7, out,
):
    nc = tc.nc
    with ExitStack() as ctx:
        lists = ctx.enter_context(tc.tile_pool(name="lists", bufs=1))
        keep = ctx.enter_context(tc.tile_pool(name="keep", bufs=1))
        psum = ctx.enter_context(tc.psum_pool(name="psum", bufs=1))

        def load_list(src, name):
            tile = lists.tile(list(src.shape), U16, name=name)
            nc.sync.dma_start(tile[:], src)
            return tile

        def load_fp8_words(tile, words):
            nc.sync.dma_start(tile[:].bitcast(I32), words[0].rearrange("p n i -> p (n i)").bitcast(I32))

        def load_row_values(src, name):
            tile = keep.tile([P, SETS], F32, name=name)
            nc.sync.dma_start(tile[:], src.rearrange("(p t) one -> p (t one)", t=SETS))
            return tile

        def zeroed_plane(width, name):
            plane = keep.tile([P, width], U8, name=name, align_bytes=64)
            nc.vector.memset(plane[:].bitcast(I32), 0)
            return plane

        def live_rows(plane, q):
            return plane[QUAD * q : QUAD * q + QROWS, :].bitcast(I32)

        def stage_scales(queue, scales, name):
            staged = keep.tile([QROWS, QUADS, scales.shape[2] // 4], I32, name=name)
            queue.dma_start(staged[:], scales[0].bitcast(I32).rearrange("(q s) c -> s q c", s=QROWS))
            return staged

        def spread_scales(plane, staged):
            for q in range(QUADS):
                nc.vector.tensor_copy(out=live_rows(plane, q), in_=staged[:, q, :])

        xt_plane = zeroed_plane(T, "xt_plane")
        w_plane = zeroed_plane(R, "w_plane")
        w2_plane = zeroed_plane(R, "w2_plane")
        boards = [keep.tile([P, C], F32, name="board%d" % t) for t in range(SETS)]
        for t, board in enumerate(boards):
            (nc.vector if t < BOARDS_ON_VECTOR else nc.gpsimd).memset(board[:].bitcast(I32), 0)
        wb_plane = zeroed_plane(N, "wb_plane")

        tokens = load_list(offs, "tokens")
        xt_staged = stage_scales(nc.scalar, xt_scales, "xt_staged")
        w_raw = keep.tile([P, R], U16, name="w_raw")
        nc.sync.dma_start(w_raw[:].bitcast(I32), w_words[0].bitcast(I32))
        w_staged = stage_scales(nc.scalar, w_scales, "w_staged")
        xt_table = keep.tile([P, T], U32, name="xt_table")
        load_fp8_words(xt_table, xt_words)

        warm = keep.tile([P, 2], F32, name="warm")
        nc.gpsimd.memset(warm[:, 0:1], 0.0)
        nc.scalar.activation(out=warm[:, 1:2], in_=warm[:, 0:1], func=ACT.Sigmoid)

        w2_staged = stage_scales(nc.sync, w2_scales, "w2_staged")
        w2_raw = keep.tile([P, R], U32, name="w2_raw")
        load_fp8_words(w2_raw, w2_words)
        board_put = load_list(offs2, "board_put")
        gate_pick = load_list(offs4, "gate_pick")
        bg_rows = load_row_values(bg, "bg_rows")
        board_pick = load_list(offs3, "board_pick")
        sa_rows = load_row_values(sa, "sa_rows")
        slot_pick = load_list(offs5, "slot_pick")
        sb_rows = load_row_values(sb, "sb_rows")
        wb_codes = keep.tile([P, N], U32, name="wb_codes", align_bytes=64)
        load_fp8_words(wb_codes, wb_words)
        page_puts = [load_list(offs6, "page_put_a"), load_list(offs7, "page_put_b")]

        spread_scales(xt_plane, xt_staged)
        spread_scales(w_plane, w_staged)
        x_scales = keep.tile([P, J], U8, name="x_scales", align_bytes=64)
        nc.vector.tensor_copy(x_scales[:], xt_plane[:].indirect(tokens[:]))
        w_dealt_scales = keep.tile([P, R], U8, name="w_dealt_scales", align_bytes=64)
        deal(nc.vector.tensor_copy, w_dealt_scales[:], w_plane[:], RUN_BYTES)
        x_codes = keep.tile([P, J], U32, name="x_codes", tag="page00", align_bytes=64)
        nc.vector.tensor_copy(x_codes[:], xt_table[:].indirect(tokens[:]))
        w_codes = keep.tile([P, R], U16, name="w_codes", tag="page01", align_bytes=64)
        deal(nc.scalar.copy, w_codes[:], w_raw[:], RUN_BYTES // 2)
        w2_first = keep.tile([P, P], U32, name="w2_first", align_bytes=64)
        deal(nc.scalar.copy, w2_first[:], w2_raw[:], RUN_BYTES // 4, 0, 1)
        w2_rest = keep.tile([P, R - P], U32, name="w2_rest", align_bytes=64)
        deal(nc.scalar.copy, w2_rest[:], w2_raw[:], RUN_BYTES // 4, 1, SETS)
        w2_codes = [w2_first[:]] + [w2_rest[:, P * t : P * (t + 1)] for t in range(SETS - 1)]
        spread_scales(w2_plane, w2_staged)
        w2_dealt_scales = keep.tile([P, R], U8, name="w2_dealt_scales", align_bytes=64)
        deal(nc.gpsimd.tensor_copy, w2_dealt_scales[:], w2_plane[:], RUN_BYTES)

        for q in range(QUADS):
            nc.sync.dma_start(live_rows(wb_plane, q), wb_scales[0, QROWS * q : QROWS * (q + 1), :].bitcast(I32))

        def first_product(codes, dealt_scales, dtype, t, bank):
            acc = psum.tile([P, J], F32, name="acc", tag="bank%d" % bank)
            nc.tensor.matmul_mx(
                out=acc[:], lhsT=codes.bitcast(dtype), lhsT_scale=dealt_scales[:, P * t : P * (t + 1)],
                rhs=x_codes[:].bitcast(E4M3X4), rhs_scale=x_scales[:], start=True, stop=True,
            )
            return acc

        a_rows = [keep.tile([P, J], F32, name="a%d" % t) for t in range(SETS)]
        b_rows = [keep.tile([P, J], F32, name="b%d" % t) for t in range(SETS)]
        picked, gates, beside = {}, {}, {}
        beside_pair0 = keep.tile([P, 2 * O], F32, name="beside_pair0")
        gated = [keep.tile([P, 2 * O], F32, name="gated%d" % h) for h in range(2)]
        diff = [keep.tile([P, 2 * O], F32, name="diff%d" % h) for h in range(2)]
        hid = keep.tile([P, O, SETS], BF16, name="hid", align_bytes=64)

        def in_pair(pair, t):
            return pair[:, O * (t % 2) : O * (t % 2 + 1)]

        def fetch_gate(t):
            gates[t] = keep.tile([P, O], F32, name="gates%d" % t, tag="board%d" % (t - 1) if t else "gates0")
            nc.scalar.activation(
                out=gates[t][:], in_=boards[t][:].indirect(gate_pick[:]), func=ACT.Sigmoid,
                bias=bg_rows[:, t : t + 1], scale=b_rows[t][:, 0:1],
            )

        def fetch_board(t):
            picked[t] = keep.tile([P, O], F32, name="picked%d" % t, tag="b%d" % (t - 1) if t else "picked0")
            nc.scalar.activation(
                out=picked[t][:], in_=boards[t][:].indirect(board_pick[:]), func=ACT.Copy, scale=sa_rows[:, t : t + 1]
            )

        def fetch_beside(t, into):
            beside[t] = into
            nc.scalar.activation(
                out=into, in_=b_rows[t][:].indirect(slot_pick[:]), func=ACT.Copy, scale=sb_rows[:, t : t + 1]
            )

        a_acc = [first_product(w_codes[:, P * t : P * (t + 1)], w_dealt_scales, E2M1X4, t, t) for t in range(SETS)]
        b_acc = [first_product(w2_codes[t], w2_dealt_scales, E5M2X4, t, SETS + t) for t in range(SETS)]

        nc.vector.tensor_copy(a_rows[0][:], a_acc[0][:])
        nc.scalar.activation(out=boards[0][:].indirect(board_put[:]), in_=a_rows[0][:], func=ACT.Copy)
        nc.vector.tensor_copy(a_rows[1][:], a_acc[1][:])
        for t in range(1, SETS):
            if t < LAST:
                nc.vector.tensor_copy(a_rows[t + 1][:], a_acc[t + 1][:])
            nc.vector.tensor_copy(boards[t][:].indirect(board_put[:]), a_rows[t][:])
        nc.vector.tensor_copy(b_rows[LAST][:], b_acc[LAST][:])

        fetch_board(0)
        for t in range(LAST):
            nc.scalar.copy(b_rows[t][:], b_acc[t][:])
            fetch_beside(t, in_pair(beside_pair0, t) if t < 2 else keep.tile([P, O], F32, name="beside%d" % t)[:])
            fetch_gate(t)
            if t > 0:
                fetch_board(t)
        fetch_board(LAST)
        fetch_gate(LAST)
        fetch_beside(LAST, keep.tile([P, O], F32, name="beside%d" % LAST, tag="board%d" % LAST)[:])

        pages = [
            [keep.tile([P, E], F32, name="page0%d" % s, align_bytes=64) for s in range(2)],
            [keep.tile([P, E], F32, name="page1%d" % s, tag="%s%d" % (rows, LAST)) for s, rows in enumerate("ab")],
        ]
        for half in pages:
            for page in half:
                nc.gpsimd.memset(page[:], 0.0)

        for t in range(2):
            nc.vector.tensor_tensor(in_pair(gated[0], t), picked[t][:], gates[t][:], ALU.mult)
        nc.vector.tensor_tensor(diff[0][:], gated[0][:], beside_pair0[:], ALU.subtract)
        for t in range(2, SETS):
            nc.vector.tensor_tensor(in_pair(gated[1], t), picked[t][:], gates[t][:], ALU.mult)
            nc.vector.tensor_tensor(in_pair(diff[1], t), in_pair(gated[1], t), beside[t], ALU.subtract)
        for h in range(2):
            nc.scalar.activation(
                out=hid[:, :, 2 * h : 2 * h + 2], in_=diff[h][:].rearrange("p (t o) -> p o t", t=2), func=ACT.Abs
            )

        hid_codes = keep.tile([P, O], U32, name="hid_codes", align_bytes=64)
        hid_scales = keep.tile([P, O], U8, name="hid_scales", align_bytes=64)
        nc.vector.quantize_mx(
            out=hid_codes[:].bitcast(E4M3X4), scales=hid_scales[:], in_=hid[:].rearrange("p o t -> p (o t)")
        )

        p_rows = []
        for h, copy in enumerate((nc.scalar.copy, nc.vector.tensor_copy)):
            acc = psum.tile([P, O], F32, name="p_acc%d" % h, tag="bank%d" % h)
            cols = slice(P * h, P * (h + 1))
            nc.tensor.matmul_mx(
                out=acc[:], lhsT=wb_codes[:, cols].bitcast(E5M2X4), lhsT_scale=wb_plane[:, cols],
                rhs=hid_codes[:].bitcast(E4M3X4), rhs_scale=hid_scales[:], start=True, stop=True,
            )
            p_rows.append(keep.tile([P, O], F32, name="p%d" % h))
            copy(p_rows[h][:], acc[:])

        for h in range(HALVES):
            nc.vector.tensor_copy(pages[h][0][:].indirect(page_puts[0][:]), p_rows[h][:])
            nc.scalar.activation(out=pages[h][1][:].indirect(page_puts[1][:]), in_=p_rows[h][:], func=ACT.Copy)

        for h in range(HALVES):
            for side in range(2):
                first_quarter = (h, side) == (0, 0)
                cols = slice(side * E // 2, (side + 1) * E // 2)
                total = keep.tile([P, E // 2], F32, name="total%d%d" % (h, side))
                adder = nc.gpsimd if first_quarter else nc.vector
                adder.tensor_tensor(total[:], pages[h][0][:, cols], pages[h][1][:, cols], ALU.add)
                queue = nc.scalar if first_quarter else nc.sync
                queue.dma_start(out[P * h : P * (h + 1), cols], total[:])
